import numpy as np
import ml_dtypes


def mxq(x, axis, fmt="e4m3"):
    dtype, down = {"e4m3": (ml_dtypes.float8_e4m3fn, 7), "e5m2": (ml_dtypes.float8_e5m2, 14)}[fmt]
    v = np.moveaxis(np.asarray(x, np.float32).astype(ml_dtypes.bfloat16).astype(np.float64), axis, -1)
    blocks = v.reshape(v.shape[:-1] + (-1, 32))
    amax = np.abs(blocks).max(-1, keepdims=True)
    byte = np.maximum(np.where(amax > 0, np.frexp(amax)[1] - 1 + 127, 0) - down, 1)
    scale = np.exp2(byte - 127.0)
    codes = (blocks / scale).astype(np.float32).astype(dtype).astype(np.float64)
    return np.moveaxis((codes * scale).reshape(v.shape), -1, axis)


WIDE = False


def mx_kscale(k):
    if not WIDE:
        return np.ones(k)
    levels = np.array([10, -10, 5, -5, 0])
    if k % 512:
        return np.exp2(np.random.permutation(np.resize(levels, k // 32))).repeat(32)
    a = np.empty((k // 512, 16))
    for p in range(k // 512):
        a[p, :8] = np.random.permutation(np.resize(levels, 8))
        for g in range(8):
            far = levels[np.abs(levels - a[p, g]) >= 10]
            a[p, g + 8] = far[np.random.randint(len(far))]
    return np.exp2(a.ravel()).repeat(32)


def f64(x):
    return np.asarray(x).astype(np.float64)


def striped(idx):
    return np.tile(idx.reshape(-1, 16).T, (8, 1)).astype(np.uint16)


def unstriped(offs):
    return offs[:16].T.reshape(-1).astype(np.int64)


def striped8(idx):
    return np.concatenate([x.reshape(-1, 16).T for x in idx]).astype(np.uint16)


def runs(offs, k):
    lists = np.stack([offs[16 * r : 16 * r + 16].T.reshape(-1) for r in range(8)]).astype(np.int64)
    return lists[np.arange(k) % 512 // 64]


def pack_weight(w):
    k, n = w.shape
    w = f64(np.asarray(w, np.float32).astype(ml_dtypes.bfloat16)).reshape(k // 32, 32, n)
    amax = np.abs(w).max(1)
    byte = np.clip(np.where(amax > 0, np.frexp(amax)[1] - 1 + 127 - 7, 1), 1, 254)
    scaled = (w * np.exp2(127.0 - byte)[:, None, :]).reshape(k, n).astype(np.float32)
    words = np.ascontiguousarray(scaled.reshape(k // 512, 128, 4, n).transpose(0, 1, 3, 2)).astype(ml_dtypes.float8_e4m3fn).view(np.uint8)
    return words, np.ascontiguousarray(byte.astype(np.uint8).reshape(k // 512, 16, n))


def unpack_weight(words, scales):
    g, p, n, _ = words.shape
    vals = np.ascontiguousarray(words).view(ml_dtypes.float8_e4m3fn).astype(np.float64) * np.repeat(np.exp2(scales.astype(np.float64) - 127.0), 8, axis=1)[..., None]
    return vals.transpose(0, 1, 3, 2).reshape(g * 512, n)


def relu(v):
    return np.maximum(v, 0.0)

def planes(y):
    n, m = y.shape
    v = y.astype(np.float32).astype(ml_dtypes.bfloat16).astype(np.float64).reshape(n // 32, 32, m)
    top = np.abs(v).max(1)
    byte = np.clip(np.where(top > 0, np.frexp(top)[1] - 1 + 127 - 7, 1), 1, 254)
    codes = (v * np.exp2(127.0 - byte)[:, None, :]).reshape(n, m).astype(np.float32).astype(ml_dtypes.float8_e4m3fn).view(np.uint8)
    words = codes.reshape(n // 512, 128, 4, m).transpose(0, 1, 3, 2)
    return np.ascontiguousarray(words), np.ascontiguousarray(byte.astype(np.uint8).reshape(n // 512, 16, m))


K, T, S, V, G, H = 512, 2048, 1024, 512, 2048, 512


def setup_inputs():
    n = np.random.standard_normal
    s = mx_kscale(K)[:, None]
    packed_xT = pack_weight(n((K, T)) * s)
    packed_dT = pack_weight(n((K, G)) / s)
    return {
        "x_words": packed_xT[0],
        "x_scales": packed_xT[1],
        "d_words": packed_dT[0],
        "d_scales": packed_dT[1],
        "gs": (np.random.uniform(0.5, 1.5, (K, 1)) * s).astype(np.float32),
        "offs": striped(np.random.permutation(T)[:S]),
        "k1": striped8(np.random.randint(0, G, (8, H))),
        "order": striped8(np.stack([np.random.permutation(S) for _ in range(8)])),
        "k2": striped8(np.random.randint(0, G, (8, H))),
    }


def reference(x_words, x_scales, d_words, d_scales, gs, offs, k1, order, k2):
    d_k2 = unpack_weight(d_words, d_scales)[np.arange(K)[:, None], runs(k2, K)]
    d_k1 = unpack_weight(d_words, d_scales)[np.arange(K)[:, None], runs(k1, K)]
    xq = unpack_weight(x_words, x_scales)[:, unstriped(offs)]
    h = 0.0625 * (d_k1.T @ xq)
    o = h[np.arange(H)[:, None], runs(order, H)]
    mx = o.reshape(H, V, 2).max(axis=2)
    z = f64(gs) * relu(mx)
    out_0 = 0.0625 * ((d_k2.T @ mxq(z, 0, "e4m3")))
    return (out_0,) + planes(out_0)

@@ -1,0 +1,165 @@
+from contextlib import ExitStack
+
+import concourse.mybir as mybir
+
+K, T, S, V, G, H = 512, 2048, 1024, 512, 2048, 512
+FLOPS = 2 * K * H * S + 2 * H * K * V
+
+F32 = mybir.dt.float32
+BF16 = mybir.dt.bfloat16
+I32 = mybir.dt.int32
+U32 = mybir.dt.uint32
+U16 = mybir.dt.uint16
+U8 = mybir.dt.uint8
+FP8X4 = mybir.dt.float8_e4m3fn_x4
+ALU = mybir.AluOpType
+ACT = mybir.ActivationFunctionType
+
+P = 128
+PACK = 4
+BANK = 512
+UNIT = 128
+CHUNKS = ((0, 384, "o0", 128), (384, 128, "z128", 128))
+
+
+def tile_picked_pqpool_relu_po_kernel(tc, x_words, x_scales, d_words, d_scales, gs, offs, k1, order, k2, out_0, out_1, out_2):
+    nc = tc.nc
+    with ExitStack() as ctx:
+        keep = ctx.enter_context(tc.tile_pool(name="keep", bufs=1))
+        hps = ctx.enter_context(tc.psum_pool(name="hps", bufs=5))
+        ops = ctx.enter_context(tc.psum_pool(name="ops", bufs=3))
+
+        def sb(name, shape, dtype, tag=""):
+            return keep.tile(shape, dtype, name=name, tag=tag or name, align_bytes=64)
+
+        k1_t = sb("k1_t", [P, H // 16], U16)
+        k2_t = sb("k2_t", [P, H // 16], U16)
+        offs_t = sb("offs_t", [P, S // 16], U16)
+        order_t = sb("order_t", [P, S // 16], U16)
+        gs_t = sb("gs_t", [P, PACK], F32)
+        ds = sb("ds", [P, G], U8)
+        xs = sb("xs", [P, T], U8)
+        dw = sb("dw", [P, G], U32)
+        xw = sb("xw", [P, T], U32)
+
+        nc.vector.memset(ds[:].bitcast(I32), 0)
+        nc.vector.memset(xs[:].bitcast(I32), 0)
+
+        nc.sync.dma_start(k1_t[:], k1)
+        ds_rows = d_scales[0].bitcast(I32).rearrange("(g e) c -> e g c", e=2)
+        for e in range(2):
+            nc.sync.dma_start(ds[:].bitcast(I32)[e:P:16, :], ds_rows[e])
+        nc.sync.dma_start(k2_t[:], k2)
+        nc.sync.dma_start(dw[:].bitcast(I32), d_words[0].rearrange("p n t -> p (n t)").bitcast(I32))
+        nc.sync.dma_start(offs_t[:], offs)
+        for q in range(4):
+            nc.sync.dma_start(xs[:].bitcast(I32)[32 * q : 32 * q + 4, :], x_scales[0].bitcast(I32)[4 * q : 4 * q + 4, :])
+        nc.sync.dma_start(xw[:].bitcast(I32), x_words[0].rearrange("p n t -> p (n t)").bitcast(I32))
+        nc.sync.dma_start(gs_t[:], gs.rearrange("(p t) o -> p (t o)", t=PACK))
+        nc.sync.dma_start(order_t[:], order)
+
+        d_s_got = sb("d_s_got", [P, 2 * H], U8)
+        nc.vector.tensor_copy(d_s_got[:, 0:H], ds[:].indirect(k1_t[:]))
+        nc.vector.tensor_copy(d_s_got[:, H : 2 * H], ds[:].indirect(k2_t[:]))
+        d_s = sb("d_s", [P, 2 * H], U8)
+        nc.vector.tensor_copy(d_s[:].rearrange("p (l t m) -> p l t m", l=2, t=PACK), d_s_got[:].rearrange("p (l m t) -> p l t m", l=2, t=PACK))
+        for e in range(2):
+            nc.scalar.dma_start(d_s[:].bitcast(I32)[2 + e : P : 32, :], d_s[:].bitcast(I32)[16 + e : P : 32, :])
+
+        def picked_words(name, lst, tag):
+            got = sb(name + "_got", [P, H], U32, tag)
+            nc.vector.tensor_copy(got[:], dw[:].indirect(lst[:]))
+            dealt = sb(name + "_dealt", [P, H], U32)
+            nc.vector.tensor_copy(dealt[:].bitcast(I32).rearrange("p (t m) -> p t m", t=PACK), got[:].bitcast(I32).rearrange("p (m t) -> p t m", t=PACK))
+            return dealt
+
+        w1 = picked_words("w1", k1_t, "")
+        xq_s = sb("xq_s", [P, S], U8)
+        nc.vector.tensor_copy(xq_s[:], xs[:].indirect(offs_t[:]))
+        xq_w = []
+        for half in range(2):
+            tw = sb("xq_w%d" % half, [P, BANK], U32)
+            nc.vector.tensor_copy(tw[:], xw[:].indirect(offs_t[:, 32 * half : 32 * half + 32]))
+            xq_w.append(tw)
+        w2 = picked_words("w2", k2_t, "xw")
+
+        gain = sb("gain", [P, PACK], F32)
+        nc.scalar.activation(gain[:], gs_t[:], ACT.Abs, scale=0.0625)
+        sign = sb("sign", [P, PACK], BF16)
+        nc.scalar.activation(sign[:], gs_t[:], ACT.Sign)
+
+        h = []
+        for t in range(PACK):
+            ht = sb("h%d" % t, [P, S], F32)
+            for half in range(2):
+                acc = hps.tile([P, BANK], F32, name="hacc")
+                nc.tensor.matmul_mx(
+                    out=acc[:],
+                    lhsT=w1[:, P * t : P * (t + 1)].bitcast(FP8X4),
+                    lhsT_scale=d_s[:, P * t : P * (t + 1)],
+                    rhs=xq_w[half][:].bitcast(FP8X4),
+                    rhs_scale=xq_s[:, BANK * half : BANK * (half + 1)],
+                    start=True,
+                    stop=True,
+                )
+                nc.scalar.activation(ht[:, BANK * half : BANK * (half + 1)], acc[:], ACT.Relu, scale=gain[:, t : t + 1])
+            h.append(ht)
+
+        y_scales = sb("y_scales", [P, V], U8)
+        out_rows = out_0.rearrange("(p t) v -> p t v", t=PACK)
+        out_words = out_1[0].rearrange("p v t -> p (v t)").bitcast(I32)
+        for v0, w, tag, part in CHUNKS:
+            o = sb("o%d" % v0, [P, PACK, 2 * w], F32, tag)
+            for t in range(PACK):
+                nc.vector.tensor_copy(o[:, t, :], h[t][:].indirect(order_t[:, v0 // 8 : (v0 + w) // 8]))
+            parts = range(0, w, part)
+            z_w, z_s = {}, {}
+            for a in parts:
+                pairs = o[:, :, 2 * a : 2 * (a + part)].rearrange("p t (c i e) -> p e c t i", i=2, e=2)
+                mag = sb("mag%d" % (v0 + a), [P, part * PACK], BF16)
+                nc.vector.tensor_tensor(mag[:].rearrange("p (c i t) -> p c t i", i=2, t=PACK), pairs[:, 0], pairs[:, 1], ALU.max)
+                z = sb("z%d" % (v0 + a), [P, part * PACK], BF16)
+                nc.vector.tensor_tensor(
+                    z[:].rearrange("p (v t) -> p v t", t=PACK),
+                    mag[:].rearrange("p (v t) -> p v t", t=PACK),
+                    sign[:].rearrange("p (a t) -> p a t", a=1).broadcast_to([P, part, PACK]),
+                    ALU.mult,
+                )
+                zw_a = sb("z_w%d" % (v0 + a), [P, part], U32)
+                zs_a = sb("z_s%d" % (v0 + a), [P, part], U8)
+                nc.vector.quantize_mx(out=zw_a[:].bitcast(FP8X4), scales=zs_a[:], in_=z[:])
+                z_w[a], z_s[a] = zw_a, zs_a
+
+            unit = min(part, UNIT)
+            y_w = sb("y_w%d" % v0, [P, w], U32)
+            for a in parts:
+                y = sb("y%d" % (v0 + a), [P, PACK, part], F32)
+                yb = sb("yb%d" % (v0 + a), [P, part * PACK], BF16)
+                for u in range(0, part, unit):
+                    acc = ops.tile([P, PACK, unit], F32, name="oacc")
+                    for t in range(PACK):
+                        nc.tensor.matmul_mx(
+                            out=acc[:, t, :],
+                            lhsT=w2[:, P * t : P * (t + 1)].bitcast(FP8X4),
+                            lhsT_scale=d_s[:, H + P * t : H + P * (t + 1)],
+                            rhs=z_w[a][:, u : u + unit].bitcast(FP8X4),
+                            rhs_scale=z_s[a][:, u : u + unit],
+                            start=True,
+                            stop=True,
+                        )
+                    nc.scalar.activation(
+                        yb[:, PACK * u : PACK * (u + unit)].rearrange("p (v t) -> p v t", t=PACK),
+                        acc[:].rearrange("p t v -> p v t"),
+                        ACT.Copy,
+                        scale=0.0625,
+                    )
+                    if part < UNIT and a == 0:
+                        nc.vector.tensor_scalar(y[:, :, u : u + unit], acc[:], 0.0625, None, ALU.mult)
+                    else:
+                        nc.scalar.activation(y[:, :, u : u + unit], acc[:], ACT.Copy, scale=0.0625)
+                nc.sync.dma_start(out_rows[:, :, v0 + a : v0 + a + part], y[:])
+                nc.vector.quantize_mx(out=y_w[:, a : a + part].bitcast(FP8X4), scales=y_scales[:, v0 + a : v0 + a + part], in_=yb[:])
+            nc.sync.dma_start(out_words[:, v0 : v0 + w], y_w[:].bitcast(I32))
+        for q in range(4):
+            eng = nc.sync if q % 2 == 0 else nc.scalar
+            eng.dma_start(out_2[0].bitcast(I32)[4 * q : 4 * q + 4, :], y_scales[:].bitcast(I32)[32 * q : 32 * q + 4, :])

@@ -19,18 +19,21 @@ P = 128
 PACK = 4
 BANK = 512
 UNIT = 128
-CHUNKS = ((0, 384, "o0", 128), (384, 128, "z128", 128))
+HALF_UNIT = 64
 
 
 def tile_picked_pqpool_relu_po_kernel(tc, x_words, x_scales, d_words, d_scales, gs, offs, k1, order, k2, out_0, out_1, out_2):
     nc = tc.nc
     with ExitStack() as ctx:
         keep = ctx.enter_context(tc.tile_pool(name="keep", bufs=1))
-        hps = ctx.enter_context(tc.psum_pool(name="hps", bufs=5))
-        ops = ctx.enter_context(tc.psum_pool(name="ops", bufs=3))
+        shared = ctx.enter_context(tc.tile_pool(name="shared", bufs=1))
+        psum = ctx.enter_context(tc.psum_pool(name="psum", bufs=8))
 
         def sb(name, shape, dtype, tag=""):
             return keep.tile(shape, dtype, name=name, tag=tag or name, align_bytes=64)
+
+        def placed(name, shape, dtype, offset):
+            return shared.tile(shape, dtype, name=name, align_bytes=64, offset=offset)
 
         k1_t = sb("k1_t", [P, H // 16], U16)
         k2_t = sb("k2_t", [P, H // 16], U16)
@@ -40,7 +43,7 @@ def tile_picked_pqpool_relu_po_kernel(tc, x_words, x_scales, d_words, d_scales, 
         ds = sb("ds", [P, G], U8)
         xs = sb("xs", [P, T], U8)
         dw = sb("dw", [P, G], U32)
-        xw = sb("xw", [P, T], U32)
+        xw = placed("xw", [P, T], U32, 512)
 
         nc.vector.memset(ds[:].bitcast(I32), 0)
         nc.vector.memset(xs[:].bitcast(I32), 0)
@@ -54,34 +57,39 @@ def tile_picked_pqpool_relu_po_kernel(tc, x_words, x_scales, d_words, d_scales, 
         nc.sync.dma_start(offs_t[:], offs)
         for q in range(4):
             nc.sync.dma_start(xs[:].bitcast(I32)[32 * q : 32 * q + 4, :], x_scales[0].bitcast(I32)[4 * q : 4 * q + 4, :])
-        nc.sync.dma_start(xw[:].bitcast(I32), x_words[0].rearrange("p n t -> p (n t)").bitcast(I32))
         nc.sync.dma_start(gs_t[:], gs.rearrange("(p t) o -> p (t o)", t=PACK))
+        nc.sync.dma_start(xw[:].bitcast(I32), x_words[0].rearrange("p n t -> p (n t)").bitcast(I32))
         nc.sync.dma_start(order_t[:], order)
 
-        d_s_got = sb("d_s_got", [P, 2 * H], U8)
-        nc.vector.tensor_copy(d_s_got[:, 0:H], ds[:].indirect(k1_t[:]))
-        nc.vector.tensor_copy(d_s_got[:, H : 2 * H], ds[:].indirect(k2_t[:]))
-        d_s = sb("d_s", [P, 2 * H], U8)
-        nc.vector.tensor_copy(d_s[:].rearrange("p (l t m) -> p l t m", l=2, t=PACK), d_s_got[:].rearrange("p (l m t) -> p l t m", l=2, t=PACK))
-        for e in range(2):
-            nc.scalar.dma_start(d_s[:].bitcast(I32)[2 + e : P : 32, :], d_s[:].bitcast(I32)[16 + e : P : 32, :])
+        def deal(dealt, got):
+            nc.vector.tensor_copy(dealt.rearrange("p (t m) -> p t m", t=PACK), got.rearrange("p (m t) -> p t m", t=PACK))
 
-        def picked_words(name, lst, tag):
-            got = sb(name + "_got", [P, H], U32, tag)
-            nc.vector.tensor_copy(got[:], dw[:].indirect(lst[:]))
-            dealt = sb(name + "_dealt", [P, H], U32)
-            nc.vector.tensor_copy(dealt[:].bitcast(I32).rearrange("p (t m) -> p t m", t=PACK), got[:].bitcast(I32).rearrange("p (m t) -> p t m", t=PACK))
-            return dealt
+        def scale_plane(plane, got):
+            deal(plane[:], got)
+            for e in range(2):
+                nc.sync.dma_start(plane[:].bitcast(I32)[2 + e : P : 32, :], plane[:].bitcast(I32)[16 + e : P : 32, :])
 
-        w1 = picked_words("w1", k1_t, "")
+        s_got = sb("s_got", [P, 2 * H], U8)
+        nc.vector.tensor_copy(s_got[:, 0:H], ds[:].indirect(k1_t[:]))
+        nc.vector.tensor_copy(s_got[:, H : 2 * H], ds[:].indirect(k2_t[:]))
+        s1 = sb("s1", [P, H], U8)
+        scale_plane(s1, s_got[:, 0:H])
+
+        w1_got = sb("w1_got", [P, H], U32)
+        nc.vector.tensor_copy(w1_got[:], dw[:].indirect(k1_t[:]))
         xq_s = sb("xq_s", [P, S], U8)
         nc.vector.tensor_copy(xq_s[:], xs[:].indirect(offs_t[:]))
+        w1 = sb("w1", [P, H], U32)
+        deal(w1[:].bitcast(I32), w1_got[:].bitcast(I32))
         xq_w = []
         for half in range(2):
             tw = sb("xq_w%d" % half, [P, BANK], U32)
             nc.vector.tensor_copy(tw[:], xw[:].indirect(offs_t[:, 32 * half : 32 * half + 32]))
             xq_w.append(tw)
-        w2 = picked_words("w2", k2_t, "xw")
+        w2_got = placed("w2_got", [P, H], U32, 3072)
+        nc.vector.tensor_copy(w2_got[:], dw[:].indirect(k2_t[:]))
+        s2 = placed("s2", [P, H], U8, 8192)
+        scale_plane(s2, s_got[:, H : 2 * H])
 
         gain = sb("gain", [P, PACK], F32)
         nc.scalar.activation(gain[:], gs_t[:], ACT.Abs, scale=0.0625)
@@ -92,11 +100,11 @@ def tile_picked_pqpool_relu_po_kernel(tc, x_words, x_scales, d_words, d_scales, 
         for t in range(PACK):
             ht = sb("h%d" % t, [P, S], F32)
             for half in range(2):
-                acc = hps.tile([P, BANK], F32, name="hacc")
+                acc = psum.tile([P, BANK], F32, name="acc")
                 nc.tensor.matmul_mx(
                     out=acc[:],
                     lhsT=w1[:, P * t : P * (t + 1)].bitcast(FP8X4),
-                    lhsT_scale=d_s[:, P * t : P * (t + 1)],
+                    lhsT_scale=s1[:, P * t : P * (t + 1)],
                     rhs=xq_w[half][:].bitcast(FP8X4),
                     rhs_scale=xq_s[:, BANK * half : BANK * (half + 1)],
                     start=True,
@@ -108,58 +116,124 @@ def tile_picked_pqpool_relu_po_kernel(tc, x_words, x_scales, d_words, d_scales, 
         y_scales = sb("y_scales", [P, V], U8)
         out_rows = out_0.rearrange("(p t) v -> p t v", t=PACK)
         out_words = out_1[0].rearrange("p v t -> p (v t)").bitcast(I32)
-        for v0, w, tag, part in CHUNKS:
-            o = sb("o%d" % v0, [P, PACK, 2 * w], F32, tag)
-            for t in range(PACK):
-                nc.vector.tensor_copy(o[:, t, :], h[t][:].indirect(order_t[:, v0 // 8 : (v0 + w) // 8]))
-            parts = range(0, w, part)
-            z_w, z_s = {}, {}
-            for a in parts:
-                pairs = o[:, :, 2 * a : 2 * (a + part)].rearrange("p t (c i e) -> p e c t i", i=2, e=2)
-                mag = sb("mag%d" % (v0 + a), [P, part * PACK], BF16)
-                nc.vector.tensor_tensor(mag[:].rearrange("p (c i t) -> p c t i", i=2, t=PACK), pairs[:, 0], pairs[:, 1], ALU.max)
-                z = sb("z%d" % (v0 + a), [P, part * PACK], BF16)
-                nc.vector.tensor_tensor(
-                    z[:].rearrange("p (v t) -> p v t", t=PACK),
-                    mag[:].rearrange("p (v t) -> p v t", t=PACK),
-                    sign[:].rearrange("p (a t) -> p a t", a=1).broadcast_to([P, part, PACK]),
-                    ALU.mult,
-                )
-                zw_a = sb("z_w%d" % (v0 + a), [P, part], U32)
-                zs_a = sb("z_s%d" % (v0 + a), [P, part], U8)
-                nc.vector.quantize_mx(out=zw_a[:].bitcast(FP8X4), scales=zs_a[:], in_=z[:])
-                z_w[a], z_s[a] = zw_a, zs_a
 
-            unit = min(part, UNIT)
-            y_w = sb("y_w%d" % v0, [P, w], U32)
-            for a in parts:
-                y = sb("y%d" % (v0 + a), [P, PACK, part], F32)
-                yb = sb("yb%d" % (v0 + a), [P, part * PACK], BF16)
-                for u in range(0, part, unit):
-                    acc = ops.tile([P, PACK, unit], F32, name="oacc")
-                    for t in range(PACK):
-                        nc.tensor.matmul_mx(
-                            out=acc[:, t, :],
-                            lhsT=w2[:, P * t : P * (t + 1)].bitcast(FP8X4),
-                            lhsT_scale=d_s[:, H + P * t : H + P * (t + 1)],
-                            rhs=z_w[a][:, u : u + unit].bitcast(FP8X4),
-                            rhs_scale=z_s[a][:, u : u + unit],
-                            start=True,
-                            stop=True,
-                        )
-                    nc.scalar.activation(
-                        yb[:, PACK * u : PACK * (u + unit)].rearrange("p (v t) -> p v t", t=PACK),
-                        acc[:].rearrange("p t v -> p v t"),
-                        ACT.Copy,
-                        scale=0.0625,
-                    )
-                    if part < UNIT and a == 0:
-                        nc.vector.tensor_scalar(y[:, :, u : u + unit], acc[:], 0.0625, None, ALU.mult)
-                    else:
-                        nc.scalar.activation(y[:, :, u : u + unit], acc[:], ACT.Copy, scale=0.0625)
-                nc.sync.dma_start(out_rows[:, :, v0 + a : v0 + a + part], y[:])
-                nc.vector.quantize_mx(out=y_w[:, a : a + part].bitcast(FP8X4), scales=y_scales[:, v0 + a : v0 + a + part], in_=yb[:])
-            nc.sync.dma_start(out_words[:, v0 : v0 + w], y_w[:].bitcast(I32))
+        def line_up(o, t, v0):
+            n = o[:].shape[2] // 2
+            nc.vector.tensor_copy(o[:, t, :], h[t][:].indirect(order_t[:, v0 // 8 : (v0 + n) // 8]))
+
+        def larger(o, a, n, v):
+            pairs = o[:, :, 2 * a : 2 * (a + n)].rearrange("p t (c i e) -> p e c t i", i=2, e=2)
+            mag = sb("mag%d" % v, [P, n * PACK], BF16)
+            nc.vector.tensor_tensor(mag[:].rearrange("p (c i t) -> p c t i", i=2, t=PACK), pairs[:, 0], pairs[:, 1], ALU.max)
+            return mag
+
+        def signed(mag, n, v):
+            z = sb("z%d" % v, [P, n * PACK], BF16)
+            nc.vector.tensor_tensor(
+                z[:].rearrange("p (v t) -> p v t", t=PACK),
+                mag[:].rearrange("p (v t) -> p v t", t=PACK),
+                sign[:].rearrange("p (a t) -> p a t", a=1).broadcast_to([P, n, PACK]),
+                ALU.mult,
+            )
+            return z
+
+        def quantised(z, n, v):
+            z_w = sb("z_w%d" % v, [P, n], U32)
+            z_s = sb("z_s%d" % v, [P, n], U8)
+            nc.vector.quantize_mx(out=z_w[:].bitcast(FP8X4), scales=z_s[:], in_=z[:])
+            return z_w, z_s
+
+        def second(zq, a, n):
+            acc = psum.tile([P, PACK, n], F32, name="acc")
+            for t in range(PACK):
+                nc.tensor.matmul_mx(
+                    out=acc[:, t, :],
+                    lhsT=w2[:, P * t : P * (t + 1)].bitcast(FP8X4),
+                    lhsT_scale=s2[:, P * t : P * (t + 1)],
+                    rhs=zq[0][:, a : a + n].bitcast(FP8X4),
+                    rhs_scale=zq[1][:, a : a + n],
+                    start=True,
+                    stop=True,
+                )
+            return acc
+
+        def rounded(yb, acc):
+            nc.scalar.activation(yb.rearrange("p (v t) -> p v t", t=PACK), acc[:].rearrange("p t v -> p v t"), ACT.Copy, scale=0.0625)
+
+        def planes(y_w, yb, v):
+            n = y_w.shape[1]
+            nc.vector.quantize_mx(out=y_w.bitcast(FP8X4), scales=y_scales[:, v : v + n], in_=yb)
+
+        va, na = 0, 2 * UNIT
+        vb, nb = na, UNIT
+        vc, ncols = na + nb, UNIT
+        o_a = sb("o_a", [P, PACK, 2 * na], F32)
+        o_b = placed("o_b", [P, PACK, 2 * nb], F32, 0)
+        o_c = placed("o_c", [P, PACK, 2 * ncols], F32, 4096)
+
+        for t in range(PACK):
+            line_up(o_a, t, va)
+        w2 = sb("w2", [P, H], U32, "gain")
+        deal(w2[:].bitcast(I32), w2_got[:].bitcast(I32))
+        mag_a = larger(o_a, 0, na, va)
+        line_up(o_b, 0, vb)
+        z_a = signed(mag_a, na, va)
+        line_up(o_b, 1, vb)
+        zq_a = quantised(z_a, na, va)
+
+        yb_a = sb("yb_a", [P, na * PACK], BF16)
+        y_a = sb("y_a", [P, PACK, na], F32)
+        accs = [second(zq_a, a, UNIT) for a in range(0, na, UNIT)]
+        for j, acc in enumerate(accs):
+            rounded(yb_a[:, PACK * UNIT * j : PACK * UNIT * (j + 1)], acc)
+        for j, acc in enumerate(accs):
+            nc.scalar.activation(y_a[:, :, UNIT * j : UNIT * (j + 1)], acc[:], ACT.Copy, scale=0.0625)
+        nc.sync.dma_start(out_rows[:, :, va : va + na], y_a[:])
+
+        line_up(o_b, 2, vb)
+        line_up(o_b, 3, vb)
+        line_up(o_c, 0, vc)
+        mag_b = larger(o_b, 0, nb, vb)
+        line_up(o_c, 1, vc)
+        z_b = signed(mag_b, nb, vb)
+        line_up(o_c, 2, vc)
+        zq_b = quantised(z_b, nb, vb)
+
+        yb_b = sb("yb_b", [P, nb * PACK], BF16)
+        y_b = sb("y_b", [P, PACK, nb], F32)
+        acc = second(zq_b, 0, nb)
+        rounded(yb_b[:], acc)
+        nc.scalar.activation(y_b[:], acc[:], ACT.Copy, scale=0.0625)
+        nc.sync.dma_start(out_rows[:, :, vb : vb + nb], y_b[:])
+
+        line_up(o_c, 3, vc)
+        yw_a = sb("yw_a", [P, na], U32)
+        planes(yw_a[:], yb_a[:], va)
+        nc.sync.dma_start(out_words[:, va : va + na], yw_a[:].bitcast(I32))
+
+        halves = range(0, ncols, HALF_UNIT)
+        mags = [larger(o_c, a, HALF_UNIT, vc + a) for a in halves]
+        zs = [signed(mag, HALF_UNIT, vc + a) for mag, a in zip(mags, halves)]
+        zqs = [quantised(z, HALF_UNIT, vc + a) for z, a in zip(zs, halves)]
+
+        yw_b = sb("yw_b", [P, nb], U32)
+        planes(yw_b[:], yb_b[:], vb)
+        nc.sync.dma_start(out_words[:, vb : vb + nb], yw_b[:].bitcast(I32))
+
+        yb_c = sb("yb_c", [P, ncols * PACK], BF16)
+        y_c = sb("y_c", [P, PACK, ncols], F32)
+        yw_c = sb("yw_c", [P, ncols], U32)
+        for zq, a in zip(zqs, halves):
+            acc = second(zq, 0, HALF_UNIT)
+            yb = yb_c[:, PACK * a : PACK * (a + HALF_UNIT)]
+            rounded(yb, acc)
+            if a == 0:
+                nc.vector.tensor_scalar(y_c[:, :, a : a + HALF_UNIT], acc[:], 0.0625, None, ALU.mult)
+            else:
+                nc.scalar.activation(y_c[:, :, a : a + HALF_UNIT], acc[:], ACT.Copy, scale=0.0625)
+            planes(yw_c[:, a : a + HALF_UNIT], yb, vc + a)
+        nc.sync.dma_start(out_rows[:, :, vc:V], y_c[:])
+        nc.scalar.dma_start(out_words[:, vc:V], yw_c[:].bitcast(I32))
         for q in range(4):
             eng = nc.sync if q % 2 == 0 else nc.scalar
             eng.dma_start(out_2[0].bitcast(I32)[4 * q : 4 * q + 4, :], y_scales[:].bitcast(I32)[32 * q : 32 * q + 4, :])

@@ -61,11 +61,11 @@ def tile_picked_pqpool_relu_po_kernel(tc, x_words, x_scales, d_words, d_scales, 
         nc.sync.dma_start(xw[:].bitcast(I32), x_words[0].rearrange("p n t -> p (n t)").bitcast(I32))
         nc.sync.dma_start(order_t[:], order)
 
-        def deal(dealt, got):
-            nc.vector.tensor_copy(dealt.rearrange("p (t m) -> p t m", t=PACK), got.rearrange("p (m t) -> p t m", t=PACK))
+        def deal(dealt, got, run):
+            nc.vector.tensor_copy(dealt.rearrange("p (t c i) -> p c t i", t=PACK, i=run), got.rearrange("p (c i t) -> p c t i", t=PACK, i=run))
 
         def scale_plane(plane, got):
-            deal(plane[:], got)
+            deal(plane[:], got, 16)
             for e in range(2):
                 nc.sync.dma_start(plane[:].bitcast(I32)[2 + e : P : 32, :], plane[:].bitcast(I32)[16 + e : P : 32, :])
 
@@ -80,7 +80,7 @@ def tile_picked_pqpool_relu_po_kernel(tc, x_words, x_scales, d_words, d_scales, 
         xq_s = sb("xq_s", [P, S], U8)
         nc.vector.tensor_copy(xq_s[:], xs[:].indirect(offs_t[:]))
         w1 = sb("w1", [P, H], U32)
-        deal(w1[:].bitcast(I32), w1_got[:].bitcast(I32))
+        deal(w1[:].bitcast(I32), w1_got[:].bitcast(I32), 4)
         xq_w = []
         for half in range(2):
             tw = sb("xq_w%d" % half, [P, BANK], U32)
@@ -96,22 +96,21 @@ def tile_picked_pqpool_relu_po_kernel(tc, x_words, x_scales, d_words, d_scales, 
         sign = sb("sign", [P, PACK], BF16)
         nc.scalar.activation(sign[:], gs_t[:], ACT.Sign)
 
-        h = []
-        for t in range(PACK):
-            ht = sb("h%d" % t, [P, S], F32)
+        h = [sb("h%d" % t, [P, S], F32) for t in range(PACK)]
+        for t0 in range(0, PACK, 2):
             for half in range(2):
-                acc = psum.tile([P, BANK], F32, name="acc")
-                nc.tensor.matmul_mx(
-                    out=acc[:],
-                    lhsT=w1[:, P * t : P * (t + 1)].bitcast(FP8X4),
-                    lhsT_scale=s1[:, P * t : P * (t + 1)],
-                    rhs=xq_w[half][:].bitcast(FP8X4),
-                    rhs_scale=xq_s[:, BANK * half : BANK * (half + 1)],
-                    start=True,
-                    stop=True,
-                )
-                nc.scalar.activation(ht[:, BANK * half : BANK * (half + 1)], acc[:], ACT.Relu, scale=gain[:, t : t + 1])
-            h.append(ht)
+                for t in (t0, t0 + 1):
+                    acc = psum.tile([P, BANK], F32, name="acc")
+                    nc.tensor.matmul_mx(
+                        out=acc[:],
+                        lhsT=w1[:, P * t : P * (t + 1)].bitcast(FP8X4),
+                        lhsT_scale=s1[:, P * t : P * (t + 1)],
+                        rhs=xq_w[half][:].bitcast(FP8X4),
+                        rhs_scale=xq_s[:, BANK * half : BANK * (half + 1)],
+                        start=True,
+                        stop=True,
+                    )
+                    nc.scalar.activation(h[t][:, BANK * half : BANK * (half + 1)], acc[:], ACT.Relu, scale=gain[:, t : t + 1])
 
         y_scales = sb("y_scales", [P, V], U8)
         out_rows = out_0.rearrange("(p t) v -> p t v", t=PACK)
@@ -122,9 +121,9 @@ def tile_picked_pqpool_relu_po_kernel(tc, x_words, x_scales, d_words, d_scales, 
             nc.vector.tensor_copy(o[:, t, :], h[t][:].indirect(order_t[:, v0 // 8 : (v0 + n) // 8]))
 
         def larger(o, a, n, v):
-            pairs = o[:, :, 2 * a : 2 * (a + n)].rearrange("p t (c i e) -> p e c t i", i=2, e=2)
+            pairs = o[:, :, 2 * a : 2 * (a + n)].rearrange("p t (c i e) -> p e c t i", i=4, e=2)
             mag = sb("mag%d" % v, [P, n * PACK], BF16)
-            nc.vector.tensor_tensor(mag[:].rearrange("p (c i t) -> p c t i", i=2, t=PACK), pairs[:, 0], pairs[:, 1], ALU.max)
+            nc.vector.tensor_tensor(mag[:].rearrange("p (c i t) -> p c t i", i=4, t=PACK), pairs[:, 0], pairs[:, 1], ALU.max)
             return mag
 
         def signed(mag, n, v):
@@ -167,14 +166,14 @@ def tile_picked_pqpool_relu_po_kernel(tc, x_words, x_scales, d_words, d_scales, 
         va, na = 0, 2 * UNIT
         vb, nb = na, UNIT
         vc, ncols = na + nb, UNIT
-        o_a = sb("o_a", [P, PACK, 2 * na], F32)
-        o_b = placed("o_b", [P, PACK, 2 * nb], F32, 0)
-        o_c = placed("o_c", [P, PACK, 2 * ncols], F32, 4096)
+        o_a = sb("o_a", [P, PACK, 2 * na], BF16)
+        o_b = placed("o_b", [P, PACK, 2 * nb], BF16, 2048)
+        o_c = placed("o_c", [P, PACK, 2 * ncols], BF16, 4096)
 
         for t in range(PACK):
             line_up(o_a, t, va)
         w2 = sb("w2", [P, H], U32, "gain")
-        deal(w2[:].bitcast(I32), w2_got[:].bitcast(I32))
+        deal(w2[:].bitcast(I32), w2_got[:].bitcast(I32), 4)
         mag_a = larger(o_a, 0, na, va)
         line_up(o_b, 0, vb)
         z_a = signed(mag_a, na, va)

@@ -49,9 +49,7 @@ def tile_picked_pqpool_relu_po_kernel(tc, x_words, x_scales, d_words, d_scales, 
         nc.vector.memset(xs[:].bitcast(I32), 0)
 
         nc.sync.dma_start(k1_t[:], k1)
-        ds_rows = d_scales[0].bitcast(I32).rearrange("(g e) c -> e g c", e=2)
-        for e in range(2):
-            nc.sync.dma_start(ds[:].bitcast(I32)[e:P:16, :], ds_rows[e])
+        nc.sync.dma_start(ds[:].bitcast(I32)[0:P:8, :], d_scales[0].bitcast(I32))
         nc.sync.dma_start(k2_t[:], k2)
         nc.sync.dma_start(dw[:].bitcast(I32), d_words[0].rearrange("p n t -> p (n t)").bitcast(I32))
         nc.sync.dma_start(offs_t[:], offs)
@@ -66,8 +64,8 @@ def tile_picked_pqpool_relu_po_kernel(tc, x_words, x_scales, d_words, d_scales, 
 
         def scale_plane(plane, got):
             deal(plane[:], got, 16)
-            for e in range(2):
-                nc.sync.dma_start(plane[:].bitcast(I32)[2 + e : P : 32, :], plane[:].bitcast(I32)[16 + e : P : 32, :])
+            for i in range(1, 4):
+                nc.sync.dma_start(plane[:].bitcast(I32)[i:P:32, :], plane[:].bitcast(I32)[8 * i : P : 32, :])
 
         s_got = sb("s_got", [P, 2 * H], U8)
         nc.vector.tensor_copy(s_got[:, 0:H], ds[:].indirect(k1_t[:]))
@@ -207,17 +205,19 @@ def tile_picked_pqpool_relu_po_kernel(tc, x_words, x_scales, d_words, d_scales, 
 
         line_up(o_c, 3, vc)
         yw_a = sb("yw_a", [P, na], U32)
-        planes(yw_a[:], yb_a[:], va)
-        nc.sync.dma_start(out_words[:, va : va + na], yw_a[:].bitcast(I32))
-
-        halves = range(0, ncols, HALF_UNIT)
-        mags = [larger(o_c, a, HALF_UNIT, vc + a) for a in halves]
-        zs = [signed(mag, HALF_UNIT, vc + a) for mag, a in zip(mags, halves)]
-        zqs = [quantised(z, HALF_UNIT, vc + a) for z, a in zip(zs, halves)]
-
         yw_b = sb("yw_b", [P, nb], U32)
+        halves = range(0, ncols, HALF_UNIT)
+        planes(yw_a[:, 0:UNIT], yb_a[:, 0 : PACK * UNIT], va)
+        mag_c0 = larger(o_c, 0, HALF_UNIT, vc)
+        planes(yw_a[:, UNIT:na], yb_a[:, PACK * UNIT : PACK * na], va + UNIT)
+        nc.sync.dma_start(out_words[:, va : va + na], yw_a[:].bitcast(I32))
+        z_c0 = signed(mag_c0, HALF_UNIT, vc)
+        mag_c1 = larger(o_c, HALF_UNIT, HALF_UNIT, vc + HALF_UNIT)
+        zq_c0 = quantised(z_c0, HALF_UNIT, vc)
+        z_c1 = signed(mag_c1, HALF_UNIT, vc + HALF_UNIT)
         planes(yw_b[:], yb_b[:], vb)
         nc.sync.dma_start(out_words[:, vb : vb + nb], yw_b[:].bitcast(I32))
+        zqs = [zq_c0, quantised(z_c1, HALF_UNIT, vc + HALF_UNIT)]
 
         yb_c = sb("yb_c", [P, ncols * PACK], BF16)
         y_c = sb("y_c", [P, PACK, ncols], F32)

from contextlib import ExitStack

import concourse.mybir as mybir

K, T, S, V, G, H = 512, 2048, 1024, 512, 2048, 512
FLOPS = 2 * K * H * S + 2 * H * K * V

F32 = mybir.dt.float32
BF16 = mybir.dt.bfloat16
I32 = mybir.dt.int32
U32 = mybir.dt.uint32
U16 = mybir.dt.uint16
U8 = mybir.dt.uint8
FP8X4 = mybir.dt.float8_e4m3fn_x4
ALU = mybir.AluOpType
ACT = mybir.ActivationFunctionType

P = 128
PACK = 4
BANK = 512
UNIT = 128
HALF_UNIT = 64


def tile_picked_pqpool_relu_po_kernel(tc, x_words, x_scales, d_words, d_scales, gs, offs, k1, order, k2, out_0, out_1, out_2):
    nc = tc.nc
    with ExitStack() as ctx:
        keep = ctx.enter_context(tc.tile_pool(name="keep", bufs=1))
        shared = ctx.enter_context(tc.tile_pool(name="shared", bufs=1))
        psum = ctx.enter_context(tc.psum_pool(name="psum", bufs=8))

        def sb(name, shape, dtype, tag=""):
            return keep.tile(shape, dtype, name=name, tag=tag or name, align_bytes=64)

        def placed(name, shape, dtype, offset):
            return shared.tile(shape, dtype, name=name, align_bytes=64, offset=offset)

        k1_t = sb("k1_t", [P, H // 16], U16)
        k2_t = sb("k2_t", [P, H // 16], U16)
        offs_t = sb("offs_t", [P, S // 16], U16)
        order_t = sb("order_t", [P, S // 16], U16)
        gs_t = sb("gs_t", [P, PACK], F32)
        ds = sb("ds", [P, G], U8)
        xs = sb("xs", [P, T], U8)
        dw = sb("dw", [P, G], U32)
        xw = placed("xw", [P, T], U32, 512)

        nc.vector.memset(ds[:].bitcast(I32), 0)
        nc.vector.memset(xs[:].bitcast(I32), 0)

        nc.sync.dma_start(k1_t[:], k1)
        nc.sync.dma_start(ds[:].bitcast(I32)[0:P:8, :], d_scales[0].bitcast(I32))
        nc.sync.dma_start(k2_t[:], k2)
        nc.sync.dma_start(dw[:].bitcast(I32), d_words[0].rearrange("p n t -> p (n t)").bitcast(I32))
        nc.sync.dma_start(offs_t[:], offs)
        for q in range(4):
            nc.sync.dma_start(xs[:].bitcast(I32)[32 * q : 32 * q + 4, :], x_scales[0].bitcast(I32)[4 * q : 4 * q + 4, :])
        nc.sync.dma_start(gs_t[:], gs.rearrange("(p t) o -> p (t o)", t=PACK))
        nc.sync.dma_start(xw[:].bitcast(I32), x_words[0].rearrange("p n t -> p (n t)").bitcast(I32))
        nc.sync.dma_start(order_t[:], order)

        def deal(dealt, got, run):
            nc.vector.tensor_copy(dealt.rearrange("p (t c i) -> p c t i", t=PACK, i=run), got.rearrange("p (c i t) -> p c t i", t=PACK, i=run))

        def scale_plane(plane, got):
            deal(plane[:], got, 16)
            for i in range(1, 4):
                nc.sync.dma_start(plane[:].bitcast(I32)[i:P:32, :], plane[:].bitcast(I32)[8 * i : P : 32, :])

        s_got = sb("s_got", [P, 2 * H], U8)
        nc.vector.tensor_copy(s_got[:, 0:H], ds[:].indirect(k1_t[:]))
        nc.vector.tensor_copy(s_got[:, H : 2 * H], ds[:].indirect(k2_t[:]))
        s1 = sb("s1", [P, H], U8)
        scale_plane(s1, s_got[:, 0:H])

        w1_got = sb("w1_got", [P, H], U32)
        nc.vector.tensor_copy(w1_got[:], dw[:].indirect(k1_t[:]))
        xq_s = sb("xq_s", [P, S], U8)
        nc.vector.tensor_copy(xq_s[:], xs[:].indirect(offs_t[:]))
        w1 = sb("w1", [P, H], U32)
        deal(w1[:].bitcast(I32), w1_got[:].bitcast(I32), 4)
        xq_w = []
        for half in range(2):
            tw = sb("xq_w%d" % half, [P, BANK], U32)
            nc.vector.tensor_copy(tw[:], xw[:].indirect(offs_t[:, 32 * half : 32 * half + 32]))
            xq_w.append(tw)
        w2_got = placed("w2_got", [P, H], U32, 3072)
        nc.vector.tensor_copy(w2_got[:], dw[:].indirect(k2_t[:]))
        s2 = placed("s2", [P, H], U8, 8192)
        scale_plane(s2, s_got[:, H : 2 * H])

        gain = sb("gain", [P, PACK], F32)
        nc.scalar.activation(gain[:], gs_t[:], ACT.Abs, scale=0.0625)
        sign = sb("sign", [P, PACK], BF16)
        nc.scalar.activation(sign[:], gs_t[:], ACT.Sign)

        h = [sb("h%d" % t, [P, S], F32) for t in range(PACK)]
        for t0 in range(0, PACK, 2):
            for half in range(2):
                for t in (t0, t0 + 1):
                    acc = psum.tile([P, BANK], F32, name="acc")
                    nc.tensor.matmul_mx(
                        out=acc[:],
                        lhsT=w1[:, P * t : P * (t + 1)].bitcast(FP8X4),
                        lhsT_scale=s1[:, P * t : P * (t + 1)],
                        rhs=xq_w[half][:].bitcast(FP8X4),
                        rhs_scale=xq_s[:, BANK * half : BANK * (half + 1)],
                        start=True,
                        stop=True,
                    )
                    nc.scalar.activation(h[t][:, BANK * half : BANK * (half + 1)], acc[:], ACT.Relu, scale=gain[:, t : t + 1])

        y_scales = sb("y_scales", [P, V], U8)
        out_rows = out_0.rearrange("(p t) v -> p t v", t=PACK)
        out_words = out_1[0].rearrange("p v t -> p (v t)").bitcast(I32)

        def line_up(o, t, v0):
            n = o[:].shape[2] // 2
            nc.vector.tensor_copy(o[:, t, :], h[t][:].indirect(order_t[:, v0 // 8 : (v0 + n) // 8]))

        def larger(o, a, n, v):
            pairs = o[:, :, 2 * a : 2 * (a + n)].rearrange("p t (c i e) -> p e c t i", i=4, e=2)
            mag = sb("mag%d" % v, [P, n * PACK], BF16)
            nc.vector.tensor_tensor(mag[:].rearrange("p (c i t) -> p c t i", i=4, t=PACK), pairs[:, 0], pairs[:, 1], ALU.max)
            return mag

        def signed(mag, n, v):
            z = sb("z%d" % v, [P, n * PACK], BF16)
            nc.vector.tensor_tensor(
                z[:].rearrange("p (v t) -> p v t", t=PACK),
                mag[:].rearrange("p (v t) -> p v t", t=PACK),
                sign[:].rearrange("p (a t) -> p a t", a=1).broadcast_to([P, n, PACK]),
                ALU.mult,
            )
            return z

        def quantised(z, n, v):
            z_w = sb("z_w%d" % v, [P, n], U32)
            z_s = sb("z_s%d" % v, [P, n], U8)
            nc.vector.quantize_mx(out=z_w[:].bitcast(FP8X4), scales=z_s[:], in_=z[:])
            return z_w, z_s

        def second(zq, a, n):
            acc = psum.tile([P, PACK, n], F32, name="acc")
            for t in range(PACK):
                nc.tensor.matmul_mx(
                    out=acc[:, t, :],
                    lhsT=w2[:, P * t : P * (t + 1)].bitcast(FP8X4),
                    lhsT_scale=s2[:, P * t : P * (t + 1)],
                    rhs=zq[0][:, a : a + n].bitcast(FP8X4),
                    rhs_scale=zq[1][:, a : a + n],
                    start=True,
                    stop=True,
                )
            return acc

        def rounded(yb, acc):
            nc.scalar.activation(yb.rearrange("p (v t) -> p v t", t=PACK), acc[:].rearrange("p t v -> p v t"), ACT.Copy, scale=0.0625)

        def planes(y_w, yb, v):
            n = y_w.shape[1]
            nc.vector.quantize_mx(out=y_w.bitcast(FP8X4), scales=y_scales[:, v : v + n], in_=yb)

        va, na = 0, 2 * UNIT
        vb, nb = na, UNIT
        vc, ncols = na + nb, UNIT
        o_a = sb("o_a", [P, PACK, 2 * na], BF16)
        o_b = placed("o_b", [P, PACK, 2 * nb], BF16, 2048)
        o_c = placed("o_c", [P, PACK, 2 * ncols], BF16, 4096)

        for t in range(PACK):
            line_up(o_a, t, va)
        w2 = sb("w2", [P, H], U32, "gain")
        deal(w2[:].bitcast(I32), w2_got[:].bitcast(I32), 4)
        mag_a = larger(o_a, 0, na, va)
        line_up(o_b, 0, vb)
        z_a = signed(mag_a, na, va)
        line_up(o_b, 1, vb)
        zq_a = quantised(z_a, na, va)

        yb_a = sb("yb_a", [P, na * PACK], BF16)
        y_a = sb("y_a", [P, PACK, na], F32)
        accs = [second(zq_a, a, UNIT) for a in range(0, na, UNIT)]
        for j, acc in enumerate(accs):
            rounded(yb_a[:, PACK * UNIT * j : PACK * UNIT * (j + 1)], acc)
        for j, acc in enumerate(accs):
            nc.scalar.activation(y_a[:, :, UNIT * j : UNIT * (j + 1)], acc[:], ACT.Copy, scale=0.0625)
        nc.sync.dma_start(out_rows[:, :, va : va + na], y_a[:])

        line_up(o_b, 2, vb)
        line_up(o_b, 3, vb)
        line_up(o_c, 0, vc)
        mag_b = larger(o_b, 0, nb, vb)
        line_up(o_c, 1, vc)
        z_b = signed(mag_b, nb, vb)
        line_up(o_c, 2, vc)
        zq_b = quantised(z_b, nb, vb)

        yb_b = sb("yb_b", [P, nb * PACK], BF16)
        y_b = sb("y_b", [P, PACK, nb], F32)
        acc = second(zq_b, 0, nb)
        rounded(yb_b[:], acc)
        nc.scalar.activation(y_b[:], acc[:], ACT.Copy, scale=0.0625)
        nc.sync.dma_start(out_rows[:, :, vb : vb + nb], y_b[:])

        line_up(o_c, 3, vc)
        yw_a = sb("yw_a", [P, na], U32)
        yw_b = sb("yw_b", [P, nb], U32)
        halves = range(0, ncols, HALF_UNIT)
        planes(yw_a[:, 0:UNIT], yb_a[:, 0 : PACK * UNIT], va)
        mag_c0 = larger(o_c, 0, HALF_UNIT, vc)
        planes(yw_a[:, UNIT:na], yb_a[:, PACK * UNIT : PACK * na], va + UNIT)
        nc.sync.dma_start(out_words[:, va : va + na], yw_a[:].bitcast(I32))
        z_c0 = signed(mag_c0, HALF_UNIT, vc)
        mag_c1 = larger(o_c, HALF_UNIT, HALF_UNIT, vc + HALF_UNIT)
        zq_c0 = quantised(z_c0, HALF_UNIT, vc)
        z_c1 = signed(mag_c1, HALF_UNIT, vc + HALF_UNIT)
        planes(yw_b[:], yb_b[:], vb)
        nc.sync.dma_start(out_words[:, vb : vb + nb], yw_b[:].bitcast(I32))
        zqs = [zq_c0, quantised(z_c1, HALF_UNIT, vc + HALF_UNIT)]

        yb_c = sb("yb_c", [P, ncols * PACK], BF16)
        y_c = sb("y_c", [P, PACK, ncols], F32)
        yw_c = sb("yw_c", [P, ncols], U32)
        for zq, a in zip(zqs, halves):
            acc = second(zq, 0, HALF_UNIT)
            yb = yb_c[:, PACK * a : PACK * (a + HALF_UNIT)]
            rounded(yb, acc)
            if a == 0:
                nc.vector.tensor_scalar(y_c[:, :, a : a + HALF_UNIT], acc[:], 0.0625, None, ALU.mult)
            else:
                nc.scalar.activation(y_c[:, :, a : a + HALF_UNIT], acc[:], ACT.Copy, scale=0.0625)
            planes(yw_c[:, a : a + HALF_UNIT], yb, vc + a)
        nc.sync.dma_start(out_rows[:, :, vc:V], y_c[:])
        nc.scalar.dma_start(out_words[:, vc:V], yw_c[:].bitcast(I32))
        for q in range(4):
            eng = nc.sync if q % 2 == 0 else nc.scalar
            eng.dma_start(out_2[0].bitcast(I32)[4 * q : 4 * q + 4, :], y_scales[:].bitcast(I32)[32 * q : 32 * q + 4, :])
